import numpy as np
import ml_dtypes


def mxq(x, axis, fmt="e4m3"):
    dtype, down = {"e4m3": (ml_dtypes.float8_e4m3fn, 7), "e5m2": (ml_dtypes.float8_e5m2, 14)}[fmt]
    v = np.moveaxis(np.asarray(x, np.float32).astype(ml_dtypes.bfloat16).astype(np.float64), axis, -1)
    blocks = v.reshape(v.shape[:-1] + (-1, 32))
    amax = np.abs(blocks).max(-1, keepdims=True)
    byte = np.maximum(np.where(amax > 0, np.frexp(amax)[1] - 1 + 127, 0) - down, 1)
    scale = np.exp2(byte - 127.0)
    codes = (blocks / scale).astype(np.float32).astype(dtype).astype(np.float64)
    return np.moveaxis((codes * scale).reshape(v.shape), -1, axis)


WIDE = False


def mx_kscale(k):
    if not WIDE:
        return np.ones(k)
    levels = np.array([10, -10, 5, -5, 0])
    if k % 512:
        return np.exp2(np.random.permutation(np.resize(levels, k // 32))).repeat(32)
    a = np.empty((k // 512, 16))
    for p in range(k // 512):
        a[p, :8] = np.random.permutation(np.resize(levels, 8))
        for g in range(8):
            far = levels[np.abs(levels - a[p, g]) >= 10]
            a[p, g + 8] = far[np.random.randint(len(far))]
    return np.exp2(a.ravel()).repeat(32)


def f64(x):
    return np.asarray(x).astype(np.float64)


def striped(idx):
    return np.tile(np.asarray(idx).reshape(-1, 16).T, (8, 1)).astype(np.uint16)


def unstriped(offs):
    return offs[:16].T.reshape(-1).astype(np.int64)


E2M1 = np.array([0.0, 0.5, 1.0, 1.5, 2.0, 3.0, 4.0, 6.0, -0.0, -0.5, -1.0, -1.5, -2.0, -3.0, -4.0, -6.0])


def pack_weight(w, fmt):
    k, n = w.shape
    w = f64(np.asarray(w, np.float32).astype(ml_dtypes.bfloat16)).reshape(k // 32, 32, n)
    amax = np.abs(w).max(1)
    if fmt == "e4m3":
        byte = np.frexp(amax)[1] - 1 + 127 - 7
    else:
        mant, ex = np.frexp(amax / 6.0)
        byte = np.where(mant > 0.5, ex, ex - 1) + 127
    byte = np.clip(np.where(amax > 0, byte, 1), 1, 254)
    scaled = (w * np.exp2(127.0 - byte)[:, None, :]).reshape(k, n).astype(np.float32)
    by_word = np.ascontiguousarray(scaled.reshape(k // 512, 128, 4, n).transpose(0, 1, 3, 2))
    if fmt == "e4m3":
        words = by_word.astype(ml_dtypes.float8_e4m3fn).view(np.uint8)
    else:
        c = by_word.astype(ml_dtypes.float4_e2m1fn).view(np.uint8) & 0xF
        words = (c[..., 0::2] | (c[..., 1::2] << 4)).reshape(k // 512, 128, 2 * n)
    return np.ascontiguousarray(words), np.ascontiguousarray(byte.astype(np.uint8).reshape(k // 512, 16, n))


def unpack_weight(words, scales, fmt):
    g, _, n = scales.shape
    words = np.ascontiguousarray(words).reshape(g, 128, n, -1)
    if fmt == "e4m3":
        vals = words.view(ml_dtypes.float8_e4m3fn).astype(np.float64)
    else:
        nib = np.empty((g, 128, n, 4), np.uint8)
        nib[..., 0::2] = words & 0xF
        nib[..., 1::2] = words >> 4
        vals = E2M1[nib]
    vals = vals * np.repeat(np.exp2(scales.astype(np.float64) - 127.0), 8, axis=1)[..., None]
    return vals.transpose(0, 1, 3, 2).reshape(g * 512, n)


def bf(x):
    return np.asarray(x, np.float32).astype(ml_dtypes.bfloat16)


def planes(Y):
    r, m = Y.shape
    b = f64(bf(Y)).reshape(r // 32, 32, m)
    amax = np.abs(b).max(1)
    byte = np.clip(np.where(amax > 0, np.frexp(amax)[1] - 1 + 127 - 7, 1), 1, 254)
    codes = (b * np.exp2(127.0 - byte)[:, None, :]).reshape(r, m).astype(np.float32).astype(ml_dtypes.float8_e4m3fn).view(np.uint8)
    words = codes.reshape(r // 512, 128, 4, m).transpose(0, 1, 3, 2)
    return np.ascontiguousarray(words), np.ascontiguousarray(byte.astype(np.uint8).reshape(r // 512, 16, m))


D, T, I, Q, E, U = 512, 2048, 512, 256, 512, 256


def setup_inputs():
    n = np.random.standard_normal
    idx = np.random.permutation(T)[:I]
    idx2 = np.random.randint(0, U, I)
    fd = mx_kscale(D)
    fi = mx_kscale(I)
    dkeysp = pack_weight(n((D, T)) * 0.7 / fd[:, None], "e2m1")
    return {
        "query": (n((D, Q)) * 0.2 / np.sqrt(D) * fd[:, None]).astype(np.float32),
        "bkeys": (n((D, U)) / fd[:, None]).astype(np.float32),
        "dkeys_words": dkeysp[0],
        "dkeys_scales": dkeysp[1],
        "size": (np.random.uniform(0.5, 2.0, (1, I)) * fi).astype(np.float32),
        "bvals": (n((E, U))).astype(np.float32),
        "dvals": (n((E, T)) * 0.7).astype(np.float32),
        "vsc": (np.random.uniform(0.5, 2.0, (I, 1)) / fi[:, None]).astype(np.float32),
        "offs": striped(idx),
        "offs2": striped(idx2),
    }


def reference(query, bkeys, dkeys_words, dkeys_scales, size, bvals, dvals, vsc, offs, offs2):
    idx = unstriped(offs)
    idx2 = unstriped(offs2)
    dkeysu = unpack_weight(dkeys_words, dkeys_scales, "e2m1")
    queryq = mxq(f64(query), 0, "e4m3")
    bkeysidx2q = mxq(f64(bkeys)[:, idx2], 0, "e4m3")
    dkeysidxg = dkeysu[:, idx]
    a = queryq.T @ bkeysidx2q + queryq.T @ dkeysidxg
    p = np.exp(a - np.max(a, axis=1, keepdims=True))
    w = p * f64(size) / np.sum(p, axis=1, keepdims=True)
    wt = w.T
    bt = f64(bvals)[:, idx2].T
    dt = f64(dvals)[:, idx].T
    vv = (bt + dt) * f64(vsc)
    vvq = mxq(vv, 0, "e4m3")
    wtq = mxq(wt, 0, "e4m3")
    o = vvq.T @ wtq
    words, scales = planes(o)
    return o, words, scales

@@ -1,0 +1,217 @@
+from contextlib import ExitStack
+
+import concourse.mybir as mybir
+from concourse.masks import make_identity
+
+D, T, I, Q, E, U = 512, 2048, 512, 256, 512, 256
+FLOPS = 2 * D * Q * I * 2 + 2 * I * E * Q
+
+F32 = mybir.dt.float32
+BF16 = mybir.dt.bfloat16
+I32 = mybir.dt.int32
+U32 = mybir.dt.uint32
+U16 = mybir.dt.uint16
+U8 = mybir.dt.uint8
+FP8X4 = mybir.dt.float8_e4m3fn_x4
+FP4X4 = mybir.dt.float4_e2m1fn_x4
+ALU = mybir.AluOpType
+ACT = mybir.ActivationFunctionType
+AXIS = mybir.AxisListType
+
+P = 128
+PACK = 4
+BV_WINDOW = I + 32
+BK_WINDOW = 3 * U
+
+
+def tile_attend_basedelta_pl_kernel(tc, query, bkeys, dkeys_words, dkeys_scales, size, bvals, dvals, vsc, offs, offs2, out_0, out_1, out_2):
+    nc = tc.nc
+    with ExitStack() as ctx:
+        sb = ctx.enter_context(tc.tile_pool(name="sb", bufs=1))
+        ps = ctx.enter_context(tc.psum_pool(name="ps", bufs=1))
+
+        def tile(name, shape, dtype):
+            return sb.tile(shape, dtype, name=name, align_bytes=64)
+
+        token_list = tile("token_list", [P, I // 16], U16)
+        base_list = tile("base_list", [P, I // 16], U16)
+        bk_raw = tile("bk_raw", [P, PACK, U], F32)
+        q_raw = tile("q_raw", [P, PACK, Q], F32)
+        dk_words = tile("dk_words", [P, T], U16)
+        dk_scales = tile("dk_scales", [P, T], U8)
+        bk_pairs = tile("bk_pairs", [P, 2 * (U + BK_WINDOW)], BF16)
+        bv_win = [tile("bv_win%d" % j, [P, BV_WINDOW], F32) for j in range(PACK)]
+        dv_win = [tile("dv_win%d" % j, [P, T], F32) for j in range(PACK)]
+        vsc_col = tile("vsc_col", [P, PACK], F32)
+        size_col = tile("size_col", [P, PACK], F32)
+        ident = tile("ident", [P, P], F32)
+
+        nc.gpsimd.memset(dk_scales[:].bitcast(U32), 0)
+        make_identity(nc, ident[:])
+        nc.vector.memset(bk_pairs[:, 4 * U :], 0.0)
+        for j in range(PACK):
+            nc.vector.memset(bv_win[j][:, U:], 0.0)
+
+        bv_planes = bvals.rearrange("(p j) u -> p j u", j=PACK)
+        dv_planes = dvals.rearrange("(p j) t -> p j t", j=PACK)
+        nc.sync.dma_start(base_list[:], offs2)
+        nc.sync.dma_start(bk_raw[:], bkeys.rearrange("(p j) u -> p j u", j=PACK))
+        nc.sync.dma_start(token_list[:], offs)
+        nc.sync.dma_start(q_raw[:], query.rearrange("(p j) q -> p j q", j=PACK))
+        nc.sync.dma_start(dk_words[:].bitcast(I32), dkeys_words[0].bitcast(I32))
+        for j in range(PACK):
+            nc.sync.dma_start(bv_win[j][:, :U], bv_planes[:, j, :])
+        for j in range(PACK):
+            nc.sync.dma_start(dv_win[j][:], dv_planes[:, j, :])
+        for quad in range(4):
+            nc.scalar.dma_start(
+                dk_scales[32 * quad : 32 * quad + 4, :].bitcast(I32),
+                dkeys_scales[0, 4 * quad : 4 * quad + 4, :].bitcast(I32),
+            )
+        nc.scalar.dma_start(size_col[:], size.rearrange("o (p t) -> p (o t)", t=PACK))
+        nc.scalar.dma_start(vsc_col[:], vsc.rearrange("(p t) o -> p (t o)", t=PACK))
+
+        nc.vector.tensor_copy(
+            bk_pairs[:, : 4 * U].rearrange("p (h u e) -> p h u e", h=2, e=2),
+            bk_raw[:].rearrange("p (h e) u -> p h u e", h=2),
+        )
+        bk_grouped = tile("bk_grouped", [P, I * PACK], BF16)
+        pair_words = bk_pairs[:].bitcast(U32)
+        for h in range(2):
+            nc.vector.tensor_copy(
+                bk_grouped[:].bitcast(U32).rearrange("p (i h) -> p i h", h=2)[:, :, h],
+                pair_words[:, h * U : h * U + BK_WINDOW].indirect(base_list[:]),
+            )
+        q_grouped = tile("q_grouped", [P, Q * PACK], BF16)
+        nc.scalar.activation(
+            q_grouped[:].rearrange("p (q t) -> p q t", t=PACK), q_raw[:].rearrange("p t q -> p q t"), ACT.Copy
+        )
+        dkg_words = tile("dkg_words", [P, I], U16)
+        dkg_scales = tile("dkg_scales", [P, I], U8)
+        nc.vector.tensor_copy(dkg_words[:], dk_words[:].indirect(token_list[:]))
+        bk_codes = tile("bk_codes", [P, I], U32)
+        bk_scales = tile("bk_scales", [P, I], U8)
+        nc.vector.quantize_mx(bk_codes[:].bitcast(FP8X4), bk_scales[:], bk_grouped[:])
+        q_codes = tile("q_codes", [P, Q], U32)
+        q_scales = tile("q_scales", [P, Q], U8)
+        nc.vector.quantize_mx(q_codes[:].bitcast(FP8X4), q_scales[:], q_grouped[:])
+        nc.vector.tensor_copy(dkg_scales[:], dk_scales[:].indirect(token_list[:]))
+
+        size_bank = ps.tile([P, PACK, P], F32, name="size_bank")
+        for t in range(PACK):
+            nc.tensor.transpose(size_bank[:, t, :], size_col[:, t : t + 1].to_broadcast([P, P]), ident[:])
+
+        vv_bank = [ps.tile([P, PACK, P], F32, name="vv_bank%d" % j) for j in range(PACK)]
+        bv_got = [tile("bv_got%d" % j, [P, I], F32) for j in range(PACK)]
+        dv_got = [tile("dv_got%d" % j, [P, I], F32) for j in range(PACK)]
+        vv_grouped = [tile("vv_grouped%d" % j, [P, P * PACK], BF16) for j in range(PACK)]
+        vv_codes = [tile("vv_codes%d" % j, [P, P], U32) for j in range(PACK)]
+        vv_scales = [tile("vv_scales%d" % j, [P, P], U8) for j in range(PACK)]
+
+        def turn(j, got, first):
+            for t in range(PACK):
+                nc.tensor.matmul(
+                    vv_bank[j][:, t, :], got[:, t::PACK], ident[:], is_transpose=True,
+                    start=(first and t == 0), stop=(not first and t == PACK - 1),
+                )
+
+        def base_values(j):
+            nc.scalar.activation(bv_got[j][:], bv_win[j][:].indirect(base_list[:]), ACT.Copy)
+            turn(j, bv_got[j], True)
+
+        def diff_values(j):
+            nc.scalar.activation(dv_got[j][:], dv_win[j][:].indirect(token_list[:]), ACT.Copy)
+            turn(j, dv_got[j], False)
+
+        def scale_values(j):
+            nc.vector.tensor_tensor(
+                vv_grouped[j][:].rearrange("p (e t) -> p e t", t=PACK),
+                vv_bank[j][:].rearrange("p t e -> p e t"),
+                vsc_col[:].unsqueeze(1).to_broadcast([P, P, PACK]),
+                ALU.mult,
+            )
+
+        def quantise_values(j):
+            nc.vector.quantize_mx(vv_codes[j][:].bitcast(FP8X4), vv_scales[j][:], vv_grouped[j][:])
+
+        base_values(0)
+        base_values(1)
+        diff_values(0)
+
+        score_bank = [ps.tile([P, I], F32, name="score%d" % b, tag="wide%d" % b) for b in range(2)]
+        for b in range(2):
+            cols = slice(b * P, (b + 1) * P)
+            nc.tensor.matmul_mx(score_bank[b][:], q_codes[:, cols].bitcast(FP8X4), q_scales[:, cols],
+                                bk_codes[:].bitcast(FP8X4), bk_scales[:], start=True, stop=False)
+            nc.tensor.matmul_mx(score_bank[b][:], q_codes[:, cols].bitcast(FP8X4), q_scales[:, cols],
+                                dkg_words[:].bitcast(FP4X4), dkg_scales[:], start=False, stop=True)
+        neg_max = [tile("neg_max%d" % b, [P, 1], F32) for b in range(2)]
+        row_sum = [tile("row_sum%d" % b, [P, 1], F32) for b in range(2)]
+        inv_sum = [tile("inv_sum%d" % b, [P, 1], F32) for b in range(2)]
+        prob = [tile("prob%d" % b, [P, I], F32) for b in range(2)]
+        weight = [tile("weight%d" % b, [P, I], BF16) for b in range(2)]
+        for b in range(2):
+            nc.vector.tensor_reduce(neg_max[b][:], score_bank[b][:], AXIS.X, ALU.max, negate=True)
+            nc.scalar.activation(prob[b][:], score_bank[b][:], ACT.Exp, bias=neg_max[b][:], accum_out=row_sum[b][:])
+        scale_values(0)
+        diff_values(1)
+        wt_bank = ps.tile([P, 2, 2, P], F32, name="wt_bank")
+        for b in range(2):
+            nc.vector.reciprocal(inv_sum[b][:], row_sum[b][:])
+            nc.vector.scalar_tensor_tensor(
+                weight[b][:].rearrange("q (p t) -> q p t", t=PACK),
+                prob[b][:].rearrange("q (p t) -> q p t", t=PACK),
+                inv_sum[b][:],
+                size_bank[:].rearrange("q t p -> q p t"),
+                ALU.mult, ALU.mult,
+            )
+            words = weight[b][:].bitcast(F32)
+            for h in range(2):
+                nc.tensor.transpose(wt_bank[:, b, h, :], words[:, h::2], ident[:])
+        quantise_values(0)
+        base_values(2)
+        scale_values(1)
+        wt_grouped = tile("wt_grouped", [P, Q * PACK], BF16)
+        nc.scalar.copy(
+            wt_grouped[:].bitcast(F32).rearrange("p (b q h) -> p b q h", b=2, h=2),
+            wt_bank[:].rearrange("p b h q -> p b q h"),
+        )
+        quantise_values(1)
+        diff_values(2)
+        wt_codes = tile("wt_codes", [P, Q], U32)
+        wt_scales = tile("wt_scales", [P, Q], U8)
+        nc.vector.quantize_mx(wt_codes[:].bitcast(FP8X4), wt_scales[:], wt_grouped[:])
+        base_values(3)
+        scale_values(2)
+        diff_values(3)
+        quantise_values(2)
+        scale_values(3)
+        quantise_values(3)
+
+        out_bank = [ps.tile([P, PACK, P], F32, name="out%d" % b, tag="wide%d" % b) for b in range(2)]
+        for j in range(PACK):
+            for b in range(2):
+                cols = slice(b * P, (b + 1) * P)
+                nc.tensor.matmul_mx(out_bank[b][:, j, :], vv_codes[j][:].bitcast(FP8X4), vv_scales[j][:],
+                                    wt_codes[:, cols].bitcast(FP8X4), wt_scales[:, cols], start=True, stop=True)
+
+        out_grouped = [tile("out_grouped%d" % b, [P, P * PACK], BF16) for b in range(2)]
+        out_f32 = [tile("out_f32_%d" % b, [P, PACK, P], F32) for b in range(2)]
+        out_codes = tile("out_codes", [P, Q], U32)
+        out_scales = tile("out_scales", [P, Q], U8)
+        nc.vector.tensor_copy(out_grouped[0][:].rearrange("p (q j) -> p q j", j=PACK), out_bank[0][:].rearrange("p j q -> p q j"))
+        nc.scalar.copy(out_grouped[1][:].rearrange("p (q j) -> p q j", j=PACK), out_bank[1][:].rearrange("p j q -> p q j"))
+        out_rows = out_0.rearrange("(p j) q -> p j q", j=PACK)
+        for b in range(2):
+            cols = slice(b * P, (b + 1) * P)
+            nc.vector.quantize_mx(out_codes[:, cols].bitcast(FP8X4), out_scales[:, cols], out_grouped[b][:])
+        for b in range(2):
+            cols = slice(b * P, (b + 1) * P)
+            nc.scalar.copy(out_f32[b][:], out_bank[b][:])
+            nc.sync.dma_start(out_rows[:, :, cols], out_f32[b][:])
+        nc.sync.dma_start(out_1[0].rearrange("p c r -> p (c r)").bitcast(I32), out_codes[:].bitcast(I32))
+        for quad in range(4):
+            nc.sync.dma_start(
+                out_2[0, 4 * quad : 4 * quad + 4, :].bitcast(I32),
+                out_scales[32 * quad : 32 * quad + 4, :].bitcast(I32),
+            )

@@ -30,8 +30,8 @@ def tile_attend_basedelta_pl_kernel(tc, query, bkeys, dkeys_words, dkeys_scales,
         sb = ctx.enter_context(tc.tile_pool(name="sb", bufs=1))
         ps = ctx.enter_context(tc.psum_pool(name="ps", bufs=1))
 
-        def tile(name, shape, dtype):
-            return sb.tile(shape, dtype, name=name, align_bytes=64)
+        def tile(name, shape, dtype, on=None):
+            return sb.tile(shape, dtype, name=name, tag=on or name, align_bytes=64)
 
         token_list = tile("token_list", [P, I // 16], U16)
         base_list = tile("base_list", [P, I // 16], U16)
@@ -46,7 +46,7 @@ def tile_attend_basedelta_pl_kernel(tc, query, bkeys, dkeys_words, dkeys_scales,
         size_col = tile("size_col", [P, PACK], F32)
         ident = tile("ident", [P, P], F32)
 
-        nc.gpsimd.memset(dk_scales[:].bitcast(U32), 0)
+        nc.vector.memset(dk_scales[:].bitcast(U32), 0)
         make_identity(nc, ident[:])
         nc.vector.memset(bk_pairs[:, 4 * U :], 0.0)
         for j in range(PACK):
@@ -55,21 +55,21 @@ def tile_attend_basedelta_pl_kernel(tc, query, bkeys, dkeys_words, dkeys_scales,
         bv_planes = bvals.rearrange("(p j) u -> p j u", j=PACK)
         dv_planes = dvals.rearrange("(p j) t -> p j t", j=PACK)
         nc.sync.dma_start(base_list[:], offs2)
-        nc.sync.dma_start(bk_raw[:], bkeys.rearrange("(p j) u -> p j u", j=PACK))
         nc.sync.dma_start(token_list[:], offs)
+        nc.sync.dma_start(size_col[:], size.rearrange("o (p t) -> p (o t)", t=PACK))
+        nc.sync.dma_start(vsc_col[:], vsc.rearrange("(p t) o -> p (t o)", t=PACK))
+        nc.sync.dma_start(bk_raw[:], bkeys.rearrange("(p j) u -> p j u", j=PACK))
         nc.sync.dma_start(q_raw[:], query.rearrange("(p j) q -> p j q", j=PACK))
-        nc.sync.dma_start(dk_words[:].bitcast(I32), dkeys_words[0].bitcast(I32))
         for j in range(PACK):
             nc.sync.dma_start(bv_win[j][:, :U], bv_planes[:, j, :])
-        for j in range(PACK):
-            nc.sync.dma_start(dv_win[j][:], dv_planes[:, j, :])
+        nc.sync.dma_start(dk_words[:].bitcast(I32), dkeys_words[0].bitcast(I32))
         for quad in range(4):
-            nc.scalar.dma_start(
+            nc.sync.dma_start(
                 dk_scales[32 * quad : 32 * quad + 4, :].bitcast(I32),
                 dkeys_scales[0, 4 * quad : 4 * quad + 4, :].bitcast(I32),
             )
-        nc.scalar.dma_start(size_col[:], size.rearrange("o (p t) -> p (o t)", t=PACK))
-        nc.scalar.dma_start(vsc_col[:], vsc.rearrange("(p t) o -> p (t o)", t=PACK))
+        for j in range(PACK):
+            nc.sync.dma_start(dv_win[j][:], dv_planes[:, j, :])
 
         nc.vector.tensor_copy(
             bk_pairs[:, : 4 * U].rearrange("p (h u e) -> p h u e", h=2, e=2),
@@ -134,8 +134,8 @@ def tile_attend_basedelta_pl_kernel(tc, query, bkeys, dkeys_words, dkeys_scales,
         def quantise_values(j):
             nc.vector.quantize_mx(vv_codes[j][:].bitcast(FP8X4), vv_scales[j][:], vv_grouped[j][:])
 
-        base_values(0)
-        base_values(1)
+        for j in range(PACK):
+            base_values(j)
         diff_values(0)
 
         score_bank = [ps.tile([P, I], F32, name="score%d" % b, tag="wide%d" % b) for b in range(2)]
@@ -148,7 +148,7 @@ def tile_attend_basedelta_pl_kernel(tc, query, bkeys, dkeys_words, dkeys_scales,
         neg_max = [tile("neg_max%d" % b, [P, 1], F32) for b in range(2)]
         row_sum = [tile("row_sum%d" % b, [P, 1], F32) for b in range(2)]
         inv_sum = [tile("inv_sum%d" % b, [P, 1], F32) for b in range(2)]
-        prob = [tile("prob%d" % b, [P, I], F32) for b in range(2)]
+        prob = [tile("prob0", [P, I], F32, on="dv_win0"), tile("prob1", [P, I], F32)]
         weight = [tile("weight%d" % b, [P, I], BF16) for b in range(2)]
         for b in range(2):
             nc.vector.tensor_reduce(neg_max[b][:], score_bank[b][:], AXIS.X, ALU.max, negate=True)
@@ -169,49 +169,56 @@ def tile_attend_basedelta_pl_kernel(tc, query, bkeys, dkeys_words, dkeys_scales,
             for h in range(2):
                 nc.tensor.transpose(wt_bank[:, b, h, :], words[:, h::2], ident[:])
         quantise_values(0)
-        base_values(2)
         scale_values(1)
-        wt_grouped = tile("wt_grouped", [P, Q * PACK], BF16)
+        diff_values(2)
+        wt_grouped = tile("wt_grouped", [P, Q * PACK], BF16, on="dv_win2")
         nc.scalar.copy(
             wt_grouped[:].bitcast(F32).rearrange("p (b q h) -> p b q h", b=2, h=2),
             wt_bank[:].rearrange("p b h q -> p b q h"),
         )
         quantise_values(1)
-        diff_values(2)
+        scale_values(2)
         wt_codes = tile("wt_codes", [P, Q], U32)
         wt_scales = tile("wt_scales", [P, Q], U8)
         nc.vector.quantize_mx(wt_codes[:].bitcast(FP8X4), wt_scales[:], wt_grouped[:])
-        base_values(3)
-        scale_values(2)
         diff_values(3)
         quantise_values(2)
-        scale_values(3)
-        quantise_values(3)
 
         out_bank = [ps.tile([P, PACK, P], F32, name="out%d" % b, tag="wide%d" % b) for b in range(2)]
-        for j in range(PACK):
+        halves = [slice(b * P, (b + 1) * P) for b in range(2)]
+
+        def product(j):
             for b in range(2):
-                cols = slice(b * P, (b + 1) * P)
                 nc.tensor.matmul_mx(out_bank[b][:, j, :], vv_codes[j][:].bitcast(FP8X4), vv_scales[j][:],
-                                    wt_codes[:, cols].bitcast(FP8X4), wt_scales[:, cols], start=True, stop=True)
+                                    wt_codes[:, halves[b]].bitcast(FP8X4), wt_scales[:, halves[b]], start=True, stop=True)
+
+        last = PACK - 1
+        out_early = tile("out_early", [P, last, Q], F32, on="dv_win3")
+        out_last = tile("out_last", [P, Q], F32)
+        out_rows = out_0.rearrange("(p j) q -> p j q", j=PACK)
+        for j in range(last):
+            product(j)
+        for b in range(2):
+            nc.scalar.copy(out_early[:, :, halves[b]], out_bank[b][:, :last, :])
+        nc.sync.dma_start(out_rows[:, :last, :], out_early[:])
+        scale_values(last)
+        quantise_values(last)
+        product(last)
 
         out_grouped = [tile("out_grouped%d" % b, [P, P * PACK], BF16) for b in range(2)]
-        out_f32 = [tile("out_f32_%d" % b, [P, PACK, P], F32) for b in range(2)]
         out_codes = tile("out_codes", [P, Q], U32)
         out_scales = tile("out_scales", [P, Q], U8)
         nc.vector.tensor_copy(out_grouped[0][:].rearrange("p (q j) -> p q j", j=PACK), out_bank[0][:].rearrange("p j q -> p q j"))
         nc.scalar.copy(out_grouped[1][:].rearrange("p (q j) -> p q j", j=PACK), out_bank[1][:].rearrange("p j q -> p q j"))
-        out_rows = out_0.rearrange("(p j) q -> p j q", j=PACK)
+        nc.vector.tensor_copy(out_last[:, halves[0]], out_bank[0][:, last, :])
+        nc.scalar.copy(out_last[:, halves[1]], out_bank[1][:, last, :])
         for b in range(2):
-            cols = slice(b * P, (b + 1) * P)
-            nc.vector.quantize_mx(out_codes[:, cols].bitcast(FP8X4), out_scales[:, cols], out_grouped[b][:])
-        for b in range(2):
-            cols = slice(b * P, (b + 1) * P)
-            nc.scalar.copy(out_f32[b][:], out_bank[b][:])
-            nc.sync.dma_start(out_rows[:, :, cols], out_f32[b][:])
+            nc.vector.quantize_mx(out_codes[:, halves[b]].bitcast(FP8X4), out_scales[:, halves[b]], out_grouped[b][:])
+        nc.scalar.dma_start(out_rows[:, last, :], out_last[:])
         nc.sync.dma_start(out_1[0].rearrange("p c r -> p (c r)").bitcast(I32), out_codes[:].bitcast(I32))
         for quad in range(4):
-            nc.sync.dma_start(
+            queue = nc.sync if quad < 2 else nc.scalar
+            queue.dma_start(
                 out_2[0, 4 * quad : 4 * quad + 4, :].bitcast(I32),
                 out_scales[32 * quad : 32 * quad + 4, :].bitcast(I32),
             )

@@ -58,29 +58,43 @@ def tile_attend_basedelta_pl_kernel(tc, query, bkeys, dkeys_words, dkeys_scales,
         nc.sync.dma_start(token_list[:], offs)
         nc.sync.dma_start(size_col[:], size.rearrange("o (p t) -> p (o t)", t=PACK))
         nc.sync.dma_start(vsc_col[:], vsc.rearrange("(p t) o -> p (t o)", t=PACK))
-        nc.sync.dma_start(bk_raw[:], bkeys.rearrange("(p j) u -> p j u", j=PACK))
-        nc.sync.dma_start(q_raw[:], query.rearrange("(p j) q -> p j q", j=PACK))
-        for j in range(PACK):
+
+        def load_base_values(j):
             nc.sync.dma_start(bv_win[j][:, :U], bv_planes[:, j, :])
+
+        def load_diff_values(j):
+            nc.sync.dma_start(dv_win[j][:], dv_planes[:, j, :])
+
+        nc.sync.dma_start(bk_raw[:], bkeys.rearrange("(p j) u -> p j u", j=PACK))
+        load_base_values(0)
+        nc.sync.dma_start(q_raw[:], query.rearrange("(p j) q -> p j q", j=PACK))
+        load_base_values(1)
         nc.sync.dma_start(dk_words[:].bitcast(I32), dkeys_words[0].bitcast(I32))
         for quad in range(4):
             nc.sync.dma_start(
                 dk_scales[32 * quad : 32 * quad + 4, :].bitcast(I32),
                 dkeys_scales[0, 4 * quad : 4 * quad + 4, :].bitcast(I32),
             )
-        for j in range(PACK):
-            nc.sync.dma_start(dv_win[j][:], dv_planes[:, j, :])
+        load_base_values(2)
+        load_diff_values(0)
+        load_base_values(3)
+        for j in range(1, PACK):
+            load_diff_values(j)
 
-        nc.vector.tensor_copy(
-            bk_pairs[:, : 4 * U].rearrange("p (h u e) -> p h u e", h=2, e=2),
-            bk_raw[:].rearrange("p (h e) u -> p h u e", h=2),
-        )
+        pair_start = [U, 0]
+
+        def pair_views(h):
+            dst = bk_pairs[:, 2 * pair_start[h] : 2 * (pair_start[h] + U)].rearrange("p (u e) -> p u e", e=2)
+            return dst, bk_raw[:, 2 * h : 2 * h + 2, :].rearrange("p e u -> p u e")
+
+        nc.vector.tensor_copy(*pair_views(0))
+        nc.scalar.activation(*pair_views(1), ACT.Copy)
         bk_grouped = tile("bk_grouped", [P, I * PACK], BF16)
         pair_words = bk_pairs[:].bitcast(U32)
         for h in range(2):
             nc.vector.tensor_copy(
                 bk_grouped[:].bitcast(U32).rearrange("p (i h) -> p i h", h=2)[:, :, h],
-                pair_words[:, h * U : h * U + BK_WINDOW].indirect(base_list[:]),
+                pair_words[:, pair_start[h] : pair_start[h] + BK_WINDOW].indirect(base_list[:]),
             )
         q_grouped = tile("q_grouped", [P, Q * PACK], BF16)
         nc.scalar.activation(
@@ -104,7 +118,7 @@ def tile_attend_basedelta_pl_kernel(tc, query, bkeys, dkeys_words, dkeys_scales,
         vv_bank = [ps.tile([P, PACK, P], F32, name="vv_bank%d" % j) for j in range(PACK)]
         bv_got = [tile("bv_got%d" % j, [P, I], F32) for j in range(PACK)]
         dv_got = [tile("dv_got%d" % j, [P, I], F32) for j in range(PACK)]
-        vv_grouped = [tile("vv_grouped%d" % j, [P, P * PACK], BF16) for j in range(PACK)]
+        vv_grouped = {}
         vv_codes = [tile("vv_codes%d" % j, [P, P], U32) for j in range(PACK)]
         vv_scales = [tile("vv_scales%d" % j, [P, P], U8) for j in range(PACK)]
 
@@ -124,6 +138,7 @@ def tile_attend_basedelta_pl_kernel(tc, query, bkeys, dkeys_words, dkeys_scales,
             turn(j, dv_got[j], False)
 
         def scale_values(j):
+            vv_grouped[j] = tile("vv_grouped%d" % j, [P, P * PACK], BF16, on="bv_win3" if j == 0 else None)
             nc.vector.tensor_tensor(
                 vv_grouped[j][:].rearrange("p (e t) -> p e t", t=PACK),
                 vv_bank[j][:].rearrange("p t e -> p e t"),
@@ -134,9 +149,10 @@ def tile_attend_basedelta_pl_kernel(tc, query, bkeys, dkeys_words, dkeys_scales,
         def quantise_values(j):
             nc.vector.quantize_mx(vv_codes[j][:].bitcast(FP8X4), vv_scales[j][:], vv_grouped[j][:])
 
-        for j in range(PACK):
+        for j in range(PACK - 1):
             base_values(j)
         diff_values(0)
+        base_values(PACK - 1)
 
         score_bank = [ps.tile([P, I], F32, name="score%d" % b, tag="wide%d" % b) for b in range(2)]
         for b in range(2):
@@ -148,19 +164,19 @@ def tile_attend_basedelta_pl_kernel(tc, query, bkeys, dkeys_words, dkeys_scales,
         neg_max = [tile("neg_max%d" % b, [P, 1], F32) for b in range(2)]
         row_sum = [tile("row_sum%d" % b, [P, 1], F32) for b in range(2)]
         inv_sum = [tile("inv_sum%d" % b, [P, 1], F32) for b in range(2)]
-        prob = [tile("prob0", [P, I], F32, on="dv_win0"), tile("prob1", [P, I], F32)]
+        prob_rows = tile("prob_rows", [P, 2, I], F32, on="bv_win3")
+        prob = [prob_rows[:, b, :] for b in range(2)]
         weight = [tile("weight%d" % b, [P, I], BF16) for b in range(2)]
         for b in range(2):
             nc.vector.tensor_reduce(neg_max[b][:], score_bank[b][:], AXIS.X, ALU.max, negate=True)
-            nc.scalar.activation(prob[b][:], score_bank[b][:], ACT.Exp, bias=neg_max[b][:], accum_out=row_sum[b][:])
-        scale_values(0)
+            nc.scalar.activation(prob[b], score_bank[b][:], ACT.Exp, bias=neg_max[b][:], accum_out=row_sum[b][:])
         diff_values(1)
         wt_bank = ps.tile([P, 2, 2, P], F32, name="wt_bank")
         for b in range(2):
             nc.vector.reciprocal(inv_sum[b][:], row_sum[b][:])
             nc.vector.scalar_tensor_tensor(
                 weight[b][:].rearrange("q (p t) -> q p t", t=PACK),
-                prob[b][:].rearrange("q (p t) -> q p t", t=PACK),
+                prob[b].rearrange("q (p t) -> q p t", t=PACK),
                 inv_sum[b][:],
                 size_bank[:].rearrange("q t p -> q p t"),
                 ALU.mult, ALU.mult,
@@ -168,8 +184,9 @@ def tile_attend_basedelta_pl_kernel(tc, query, bkeys, dkeys_words, dkeys_scales,
             words = weight[b][:].bitcast(F32)
             for h in range(2):
                 nc.tensor.transpose(wt_bank[:, b, h, :], words[:, h::2], ident[:])
-        quantise_values(0)
+        scale_values(0)
         scale_values(1)
+        quantise_values(0)
         diff_values(2)
         wt_grouped = tile("wt_grouped", [P, Q * PACK], BF16, on="dv_win2")
         nc.scalar.copy(

from contextlib import ExitStack

import concourse.mybir as mybir
from concourse.masks import make_identity

D, T, I, Q, E, U = 512, 2048, 512, 256, 512, 256
FLOPS = 2 * D * Q * I * 2 + 2 * I * E * Q

F32 = mybir.dt.float32
BF16 = mybir.dt.bfloat16
I32 = mybir.dt.int32
U32 = mybir.dt.uint32
U16 = mybir.dt.uint16
U8 = mybir.dt.uint8
FP8X4 = mybir.dt.float8_e4m3fn_x4
FP4X4 = mybir.dt.float4_e2m1fn_x4
ALU = mybir.AluOpType
ACT = mybir.ActivationFunctionType
AXIS = mybir.AxisListType

P = 128
PACK = 4
BV_WINDOW = I + 32
BK_WINDOW = 3 * U


def tile_attend_basedelta_pl_kernel(tc, query, bkeys, dkeys_words, dkeys_scales, size, bvals, dvals, vsc, offs, offs2, out_0, out_1, out_2):
    nc = tc.nc
    with ExitStack() as ctx:
        sb = ctx.enter_context(tc.tile_pool(name="sb", bufs=1))
        ps = ctx.enter_context(tc.psum_pool(name="ps", bufs=1))

        def tile(name, shape, dtype, on=None):
            return sb.tile(shape, dtype, name=name, tag=on or name, align_bytes=64)

        token_list = tile("token_list", [P, I // 16], U16)
        base_list = tile("base_list", [P, I // 16], U16)
        bk_raw = tile("bk_raw", [P, PACK, U], F32)
        q_raw = tile("q_raw", [P, PACK, Q], F32)
        dk_words = tile("dk_words", [P, T], U16)
        dk_scales = tile("dk_scales", [P, T], U8)
        bk_pairs = tile("bk_pairs", [P, 2 * (U + BK_WINDOW)], BF16)
        bv_win = [tile("bv_win%d" % j, [P, BV_WINDOW], F32) for j in range(PACK)]
        dv_win = [tile("dv_win%d" % j, [P, T], F32) for j in range(PACK)]
        vsc_col = tile("vsc_col", [P, PACK], F32)
        size_col = tile("size_col", [P, PACK], F32)
        ident = tile("ident", [P, P], F32)

        nc.vector.memset(dk_scales[:].bitcast(U32), 0)
        make_identity(nc, ident[:])
        nc.vector.memset(bk_pairs[:, 4 * U :], 0.0)
        for j in range(PACK):
            nc.vector.memset(bv_win[j][:, U:], 0.0)

        bv_planes = bvals.rearrange("(p j) u -> p j u", j=PACK)
        dv_planes = dvals.rearrange("(p j) t -> p j t", j=PACK)
        nc.sync.dma_start(base_list[:], offs2)
        nc.sync.dma_start(token_list[:], offs)
        nc.sync.dma_start(size_col[:], size.rearrange("o (p t) -> p (o t)", t=PACK))
        nc.sync.dma_start(vsc_col[:], vsc.rearrange("(p t) o -> p (t o)", t=PACK))

        def load_base_values(j):
            nc.sync.dma_start(bv_win[j][:, :U], bv_planes[:, j, :])

        def load_diff_values(j):
            nc.sync.dma_start(dv_win[j][:], dv_planes[:, j, :])

        nc.sync.dma_start(bk_raw[:], bkeys.rearrange("(p j) u -> p j u", j=PACK))
        load_base_values(0)
        nc.sync.dma_start(q_raw[:], query.rearrange("(p j) q -> p j q", j=PACK))
        load_base_values(1)
        nc.sync.dma_start(dk_words[:].bitcast(I32), dkeys_words[0].bitcast(I32))
        for quad in range(4):
            nc.sync.dma_start(
                dk_scales[32 * quad : 32 * quad + 4, :].bitcast(I32),
                dkeys_scales[0, 4 * quad : 4 * quad + 4, :].bitcast(I32),
            )
        load_base_values(2)
        load_diff_values(0)
        load_base_values(3)
        for j in range(1, PACK):
            load_diff_values(j)

        pair_start = [U, 0]

        def pair_views(h):
            dst = bk_pairs[:, 2 * pair_start[h] : 2 * (pair_start[h] + U)].rearrange("p (u e) -> p u e", e=2)
            return dst, bk_raw[:, 2 * h : 2 * h + 2, :].rearrange("p e u -> p u e")

        nc.vector.tensor_copy(*pair_views(0))
        nc.scalar.activation(*pair_views(1), ACT.Copy)
        bk_grouped = tile("bk_grouped", [P, I * PACK], BF16)
        pair_words = bk_pairs[:].bitcast(U32)
        for h in range(2):
            nc.vector.tensor_copy(
                bk_grouped[:].bitcast(U32).rearrange("p (i h) -> p i h", h=2)[:, :, h],
                pair_words[:, pair_start[h] : pair_start[h] + BK_WINDOW].indirect(base_list[:]),
            )
        q_grouped = tile("q_grouped", [P, Q * PACK], BF16)
        nc.scalar.activation(
            q_grouped[:].rearrange("p (q t) -> p q t", t=PACK), q_raw[:].rearrange("p t q -> p q t"), ACT.Copy
        )
        dkg_words = tile("dkg_words", [P, I], U16)
        dkg_scales = tile("dkg_scales", [P, I], U8)
        nc.vector.tensor_copy(dkg_words[:], dk_words[:].indirect(token_list[:]))
        bk_codes = tile("bk_codes", [P, I], U32)
        bk_scales = tile("bk_scales", [P, I], U8)
        nc.vector.quantize_mx(bk_codes[:].bitcast(FP8X4), bk_scales[:], bk_grouped[:])
        q_codes = tile("q_codes", [P, Q], U32)
        q_scales = tile("q_scales", [P, Q], U8)
        nc.vector.quantize_mx(q_codes[:].bitcast(FP8X4), q_scales[:], q_grouped[:])
        nc.vector.tensor_copy(dkg_scales[:], dk_scales[:].indirect(token_list[:]))

        size_bank = ps.tile([P, PACK, P], F32, name="size_bank")
        for t in range(PACK):
            nc.tensor.transpose(size_bank[:, t, :], size_col[:, t : t + 1].to_broadcast([P, P]), ident[:])

        vv_bank = [ps.tile([P, PACK, P], F32, name="vv_bank%d" % j) for j in range(PACK)]
        bv_got = [tile("bv_got%d" % j, [P, I], F32) for j in range(PACK)]
        dv_got = [tile("dv_got%d" % j, [P, I], F32) for j in range(PACK)]
        vv_grouped = {}
        vv_codes = [tile("vv_codes%d" % j, [P, P], U32) for j in range(PACK)]
        vv_scales = [tile("vv_scales%d" % j, [P, P], U8) for j in range(PACK)]

        def turn(j, got, first):
            for t in range(PACK):
                nc.tensor.matmul(
                    vv_bank[j][:, t, :], got[:, t::PACK], ident[:], is_transpose=True,
                    start=(first and t == 0), stop=(not first and t == PACK - 1),
                )

        def base_values(j):
            nc.scalar.activation(bv_got[j][:], bv_win[j][:].indirect(base_list[:]), ACT.Copy)
            turn(j, bv_got[j], True)

        def diff_values(j):
            nc.scalar.activation(dv_got[j][:], dv_win[j][:].indirect(token_list[:]), ACT.Copy)
            turn(j, dv_got[j], False)

        def scale_values(j):
            vv_grouped[j] = tile("vv_grouped%d" % j, [P, P * PACK], BF16, on="bv_win3" if j == 0 else None)
            nc.vector.tensor_tensor(
                vv_grouped[j][:].rearrange("p (e t) -> p e t", t=PACK),
                vv_bank[j][:].rearrange("p t e -> p e t"),
                vsc_col[:].unsqueeze(1).to_broadcast([P, P, PACK]),
                ALU.mult,
            )

        def quantise_values(j):
            nc.vector.quantize_mx(vv_codes[j][:].bitcast(FP8X4), vv_scales[j][:], vv_grouped[j][:])

        for j in range(PACK - 1):
            base_values(j)
        diff_values(0)
        base_values(PACK - 1)

        score_bank = [ps.tile([P, I], F32, name="score%d" % b, tag="wide%d" % b) for b in range(2)]
        for b in range(2):
            cols = slice(b * P, (b + 1) * P)
            nc.tensor.matmul_mx(score_bank[b][:], q_codes[:, cols].bitcast(FP8X4), q_scales[:, cols],
                                bk_codes[:].bitcast(FP8X4), bk_scales[:], start=True, stop=False)
            nc.tensor.matmul_mx(score_bank[b][:], q_codes[:, cols].bitcast(FP8X4), q_scales[:, cols],
                                dkg_words[:].bitcast(FP4X4), dkg_scales[:], start=False, stop=True)
        neg_max = [tile("neg_max%d" % b, [P, 1], F32) for b in range(2)]
        row_sum = [tile("row_sum%d" % b, [P, 1], F32) for b in range(2)]
        inv_sum = [tile("inv_sum%d" % b, [P, 1], F32) for b in range(2)]
        prob_rows = tile("prob_rows", [P, 2, I], F32, on="bv_win3")
        prob = [prob_rows[:, b, :] for b in range(2)]
        weight = [tile("weight%d" % b, [P, I], BF16) for b in range(2)]
        for b in range(2):
            nc.vector.tensor_reduce(neg_max[b][:], score_bank[b][:], AXIS.X, ALU.max, negate=True)
            nc.scalar.activation(prob[b], score_bank[b][:], ACT.Exp, bias=neg_max[b][:], accum_out=row_sum[b][:])
        diff_values(1)
        wt_bank = ps.tile([P, 2, 2, P], F32, name="wt_bank")
        for b in range(2):
            nc.vector.reciprocal(inv_sum[b][:], row_sum[b][:])
            nc.vector.scalar_tensor_tensor(
                weight[b][:].rearrange("q (p t) -> q p t", t=PACK),
                prob[b].rearrange("q (p t) -> q p t", t=PACK),
                inv_sum[b][:],
                size_bank[:].rearrange("q t p -> q p t"),
                ALU.mult, ALU.mult,
            )
            words = weight[b][:].bitcast(F32)
            for h in range(2):
                nc.tensor.transpose(wt_bank[:, b, h, :], words[:, h::2], ident[:])
        scale_values(0)
        scale_values(1)
        quantise_values(0)
        diff_values(2)
        wt_grouped = tile("wt_grouped", [P, Q * PACK], BF16, on="dv_win2")
        nc.scalar.copy(
            wt_grouped[:].bitcast(F32).rearrange("p (b q h) -> p b q h", b=2, h=2),
            wt_bank[:].rearrange("p b h q -> p b q h"),
        )
        quantise_values(1)
        scale_values(2)
        wt_codes = tile("wt_codes", [P, Q], U32)
        wt_scales = tile("wt_scales", [P, Q], U8)
        nc.vector.quantize_mx(wt_codes[:].bitcast(FP8X4), wt_scales[:], wt_grouped[:])
        diff_values(3)
        quantise_values(2)

        out_bank = [ps.tile([P, PACK, P], F32, name="out%d" % b, tag="wide%d" % b) for b in range(2)]
        halves = [slice(b * P, (b + 1) * P) for b in range(2)]

        def product(j):
            for b in range(2):
                nc.tensor.matmul_mx(out_bank[b][:, j, :], vv_codes[j][:].bitcast(FP8X4), vv_scales[j][:],
                                    wt_codes[:, halves[b]].bitcast(FP8X4), wt_scales[:, halves[b]], start=True, stop=True)

        last = PACK - 1
        out_early = tile("out_early", [P, last, Q], F32, on="dv_win3")
        out_last = tile("out_last", [P, Q], F32)
        out_rows = out_0.rearrange("(p j) q -> p j q", j=PACK)
        for j in range(last):
            product(j)
        for b in range(2):
            nc.scalar.copy(out_early[:, :, halves[b]], out_bank[b][:, :last, :])
        nc.sync.dma_start(out_rows[:, :last, :], out_early[:])
        scale_values(last)
        quantise_values(last)
        product(last)

        out_grouped = [tile("out_grouped%d" % b, [P, P * PACK], BF16) for b in range(2)]
        out_codes = tile("out_codes", [P, Q], U32)
        out_scales = tile("out_scales", [P, Q], U8)
        nc.vector.tensor_copy(out_grouped[0][:].rearrange("p (q j) -> p q j", j=PACK), out_bank[0][:].rearrange("p j q -> p q j"))
        nc.scalar.copy(out_grouped[1][:].rearrange("p (q j) -> p q j", j=PACK), out_bank[1][:].rearrange("p j q -> p q j"))
        nc.vector.tensor_copy(out_last[:, halves[0]], out_bank[0][:, last, :])
        nc.scalar.copy(out_last[:, halves[1]], out_bank[1][:, last, :])
        for b in range(2):
            nc.vector.quantize_mx(out_codes[:, halves[b]].bitcast(FP8X4), out_scales[:, halves[b]], out_grouped[b][:])
        nc.scalar.dma_start(out_rows[:, last, :], out_last[:])
        nc.sync.dma_start(out_1[0].rearrange("p c r -> p (c r)").bitcast(I32), out_codes[:].bitcast(I32))
        for quad in range(4):
            queue = nc.sync if quad < 2 else nc.scalar
            queue.dma_start(
                out_2[0, 4 * quad : 4 * quad + 4, :].bitcast(I32),
                out_scales[32 * quad : 32 * quad + 4, :].bitcast(I32),
            )
